import numpy as np
import ml_dtypes


def mxq(x, axis, fmt="e4m3"):
    dtype, down = {"e4m3": (ml_dtypes.float8_e4m3fn, 7), "e5m2": (ml_dtypes.float8_e5m2, 14)}[fmt]
    v = np.moveaxis(np.asarray(x, np.float32).astype(ml_dtypes.bfloat16).astype(np.float64), axis, -1)
    blocks = v.reshape(v.shape[:-1] + (-1, 32))
    amax = np.abs(blocks).max(-1, keepdims=True)
    byte = np.maximum(np.where(amax > 0, np.frexp(amax)[1] - 1 + 127, 0) - down, 1)
    scale = np.exp2(byte - 127.0)
    codes = (blocks / scale).astype(np.float32).astype(dtype).astype(np.float64)
    return np.moveaxis((codes * scale).reshape(v.shape), -1, axis)


WIDE = False


def mx_kscale(k):
    if not WIDE:
        return np.ones(k)
    levels = np.array([10, -10, 5, -5, 0])
    if k % 512:
        return np.exp2(np.random.permutation(np.resize(levels, k // 32))).repeat(32)
    a = np.empty((k // 512, 16))
    for p in range(k // 512):
        a[p, :8] = np.random.permutation(np.resize(levels, 8))
        for g in range(8):
            far = levels[np.abs(levels - a[p, g]) >= 10]
            a[p, g + 8] = far[np.random.randint(len(far))]
    return np.exp2(a.ravel()).repeat(32)


BF16 = ml_dtypes.bfloat16


def bf(x):
    return np.asarray(x, np.float32).astype(BF16)


def f64(x):
    return np.asarray(x).astype(np.float64)


E2M1 = np.array([0.0, 0.5, 1.0, 1.5, 2.0, 3.0, 4.0, 6.0, -0.0, -0.5, -1.0, -1.5, -2.0, -3.0, -4.0, -6.0])


def pack_weight(w, fmt):
    k, n = w.shape
    w = f64(bf(w)).reshape(k // 32, 32, n)
    amax = np.abs(w).max(1)
    if fmt == "e4m3":
        byte = np.frexp(amax)[1] - 1 + 127 - 7
    else:
        mant, ex = np.frexp(amax / 6.0)
        byte = np.where(mant > 0.5, ex, ex - 1) + 127
    byte = np.clip(np.where(amax > 0, byte, 1), 1, 254)
    scaled = (w * np.exp2(127.0 - byte)[:, None, :]).reshape(k, n).astype(np.float32)
    by_word = np.ascontiguousarray(scaled.reshape(k // 512, 128, 4, n).transpose(0, 1, 3, 2))
    if fmt == "e4m3":
        words = by_word.astype(ml_dtypes.float8_e4m3fn).view(np.uint8)
    else:
        c = by_word.astype(ml_dtypes.float4_e2m1fn).view(np.uint8) & 0xF
        words = c[..., 0::2] | (c[..., 1::2] << 4)
    return np.ascontiguousarray(words), np.ascontiguousarray(byte.astype(np.uint8).reshape(k // 512, 16, n))


def unpack_weight(words, scales, fmt):
    g, p, n, _ = words.shape
    if fmt == "e4m3":
        vals = np.ascontiguousarray(words).view(ml_dtypes.float8_e4m3fn).astype(np.float64)
    else:
        nib = np.empty((g, p, n, 4), np.uint8)
        nib[..., 0::2] = words & 0xF
        nib[..., 1::2] = words >> 4
        vals = E2M1[nib]
    vals = vals * np.repeat(np.exp2(scales.astype(np.float64) - 127.0), 8, axis=1)[..., None]
    return vals.transpose(0, 1, 3, 2).reshape(g * 512, n)
def pack4(w):
    words, scales = pack_weight(w, "e2m1")
    return words.reshape(words.shape[0], 128, -1), scales


def unpack4(words, scales):
    return unpack_weight(words.reshape(words.shape[0], 128, -1, 2), scales, "e2m1")


M, D, F = 1024, 1024, 2048

HALF = 0.5


def swish(a):
    return a * (0.5 + 0.5 * np.tanh(0.5 * a))


def setup_inputs():
    s, t = mx_kscale(D), mx_kscale(F)
    loud = np.exp(0.3 * np.random.standard_normal((M, 1)))
    x = bf(loud * (np.random.standard_normal((M, D)) + 0.3 * np.random.standard_normal((M, 1))))
    x4_words, x4_scales = pack4(f64(x).T * s[:, None])
    w1_words, w1_scales = pack4(np.random.standard_normal((D, F)) / np.sqrt(D) / s[:, None])
    w2_words, w2_scales = pack4(2.0 * np.random.standard_normal((F, D)) / np.sqrt(F) / t[:, None])
    return {"x": x,
            "x4_words": x4_words, "x4_scales": x4_scales,
            "w1_words": w1_words, "w1_scales": w1_scales,
            "b1": bf(0.3 * np.random.standard_normal(F)),
            "c": bf((1.0 + 0.3 * np.random.standard_normal(F)) * t),
            "w2_words": w2_words, "w2_scales": w2_scales,
            "b2": bf(0.5 * np.random.standard_normal(D)),
            "gain": bf(1.0 + 0.1 * np.random.standard_normal(D)),
            "beta": bf(0.3 * np.random.standard_normal(D))}


def reference(x, x4_words, x4_scales, w1_words, w1_scales, b1, c, w2_words, w2_scales, b2, gain, beta):
    xr = f64(x)
    a4 = unpack4(x4_words, x4_scales)
    w1 = unpack4(w1_words, w1_scales)
    w2 = unpack4(w2_words, w2_scales)
    rho = 1.0 / np.sqrt(np.mean(xr * xr, axis=1, keepdims=True))
    u = a4.T @ w1
    h = swish(rho * u + f64(b1)) * f64(c)
    y = (mxq(h, 1, "e4m3") @ w2) + f64(b2)
    z = xr + HALF * y
    zc = z - np.mean(z, axis=1, keepdims=True)
    return zc / np.sqrt(np.mean(zc * zc, axis=1, keepdims=True)) * f64(gain) + f64(beta)

from contextlib import ExitStack

import concourse.mybir as mybir
from concourse.masks import make_identity

M, D, F = 1024, 1024, 2048
FLOPS = 2 * M * D * F * 2

F32 = mybir.dt.float32
BF16 = mybir.dt.bfloat16
I32 = mybir.dt.int32
U32 = mybir.dt.uint32
U8 = mybir.dt.uint8
FP4 = mybir.dt.float4_e2m1fn_x4
FP8 = mybir.dt.float8_e4m3fn_x4
ACT = mybir.ActivationFunctionType
ALU = mybir.AluOpType

P = 128
K1 = D // 512
G = F // 512
TILES = M // P
BLOCKS = [[0,256],[256,256],[512,256],[768,128],[896,128]]
ON_VECTOR = [6,7]
GP_STEPS = []


def tile_conformer_swish_half_step_f2_kernel(
    tc, x, x4_words, x4_scales, w1_words, w1_scales, b1, c, w2_words, w2_scales, b2, gain, beta, out
):
    nc = tc.nc
    with ExitStack() as ctx:
        keep = ctx.enter_context(tc.tile_pool(name="keep", bufs=1))
        work = ctx.enter_context(tc.tile_pool(name="work", bufs=3))
        upool = ctx.enter_context(tc.psum_pool(name="upool", bufs=3))
        ypool = ctx.enter_context(tc.psum_pool(name="ypool", bufs=3))
        cpool = ctx.enter_context(tc.psum_pool(name="cpool", bufs=1))

        x_sb = keep.tile([P, TILES, D], BF16, align_bytes=64)
        xb = keep.tile([P, TILES, D], F32, align_bytes=64)
        x4_sb = keep.tile([P, 2, K1, M], U8, align_bytes=64)
        x4s = keep.tile([P, K1, M], U8, align_bytes=64)
        w1_raw = keep.tile([P, G, K1, 1024], U8, align_bytes=64)
        w1s_raw = keep.tile([P, K1, F], U8, align_bytes=64)
        w1_st = keep.tile([P, G, K1, 1024], U8, align_bytes=64)
        w1s_st = keep.tile([P, G, K1, 512], U8, align_bytes=64)
        w2_sb = keep.tile([P, G, 2 * D], U8, align_bytes=64)
        w2s = keep.tile([P, G, D], U8, align_bytes=64)
        b1_sb = keep.tile([P, G, 4], BF16, align_bytes=64)
        c_sb = keep.tile([P, G, 4], BF16, align_bytes=64)
        c32 = keep.tile([P, G, 4], F32, align_bytes=64)
        rows = keep.tile([P, 3, D], BF16, align_bytes=64)
        sel = keep.tile([P, 3, P], BF16, align_bytes=64)
        b2h = keep.tile([P, D], F32, align_bytes=64)
        beta_bc = keep.tile([P, D], BF16, align_bytes=64)
        ident = keep.tile([P, P], F32, align_bytes=64)
        ident16 = keep.tile([P, P], BF16, align_bytes=64)
        expo = keep.tile([P, 8], F32, align_bytes=64)
        ssq = keep.tile([P, 8], F32, align_bytes=64)
        rho = keep.tile([P, 8], F32, align_bytes=64)
        rho_bc = keep.tile([P, M], F32, align_bytes=64)
        warm = keep.tile([P, 8], F32, align_bytes=64)
        gain_ps = cpool.tile([P, D], BF16)
        c_ps = cpool.tile([P, G, 4], F32)

        def words(ap):
            return ap.bitcast(I32)

        nc.vector.memset(words(w1s_raw[:].rearrange("p k n -> p (k n)")), 0)
        nc.vector.memset(words(x4s[:].rearrange("p k n -> p (k n)")), 0)
        nc.gpsimd.memset(expo[:], -0.5)
        make_identity(nc, ident[:])
        nc.gpsimd.memset(rows[:].rearrange("p r n -> p (r n)").bitcast(I32), 0)
        nc.gpsimd.memset(sel[:].rearrange("p r n -> p (r n)").bitcast(I32), 0)
        nc.gpsimd.memset(sel[0:1, 0, :], 0.5)
        nc.gpsimd.memset(sel[0:1, 1, :], 32.0)
        nc.gpsimd.memset(sel[0:1, 2, :], 1.0)
        nc.gpsimd.memset(words(w2s[:].rearrange("p g n -> p (g n)")), 0)
        nc.vector.memset(warm[:], 0.0)
        nc.scalar.activation(out=warm[:, 0:1], in_=warm[:, 1:2], func=ACT.Silu)

        x_v = x.rearrange("(j p) d -> p j d", p=P)
        out_v = out.rearrange("(j p) d -> p j d", p=P)
        w1_v = w1_words.rearrange("k p b -> p k b")
        x4_v = x4_words.rearrange("k p b -> p k b")
        w2_v = w2_words.rearrange("k p b -> p k b")

        def load_w1(g):
            nc.sync.dma_start(out=words(w1_raw[:, g, :, :]), in_=words(w1_v[:, :, 1024 * g : 1024 * g + 1024]))

        def load_x4(h):
            nc.sync.dma_start(out=words(x4_sb[:, h, :, :]), in_=words(x4_v[:, :, 1024 * h : 1024 * h + 1024]))

        def load_x(j0, j1):
            nc.sync.dma_start(out=x_sb[:, j0:j1, :], in_=x_v[:, j0:j1, :])

        def load_scales(plane, src):
            for q in range(4):
                nc.sync.dma_start(
                    out=words(plane[32 * q : 32 * q + 4, :, :]),
                    in_=words(src[:, 4 * q : 4 * q + 4, :].rearrange("k r n -> r k n")),
                )

        nc.scalar.dma_start(out=b1_sb[:], in_=b1.rearrange("(g p t) -> p g t", p=P, t=4))
        nc.scalar.dma_start(out=c_sb[:], in_=c.rearrange("(g p t) -> p g t", p=P, t=4))
        load_x(0, 1)
        load_x(1, 2)
        load_w1(0)
        load_x4(0)
        load_scales(w1s_raw, w1_scales)
        load_scales(x4s, x4_scales)
        load_w1(1)
        for r, vec in enumerate((b2, gain, beta)):
            nc.sync.dma_start(out=rows[0:1, r, :], in_=vec.rearrange("(o n) -> o n", o=1))
        load_w1(2)
        load_w1(3)
        load_x(2, 4)
        nc.sync.dma_start(out=words(w2_sb[:]), in_=words(w2_v))
        load_scales(w2s, w2_scales)
        load_x4(1)
        load_x(4, 8)

        def permute_w1(g):
            for k in range(K1):
                nc.vector.tensor_copy(
                    out=w1_st[:, g, k, :].rearrange("p (t q b) -> p t q b", t=4, b=2),
                    in_=w1_raw[:, g, k, :].rearrange("p (q t b) -> p t q b", t=4, b=2),
                )
            cols = slice(512 * g, 512 * g + 512)
            nc.vector.tensor_copy(
                out=w1s_st[:, g, :, :].rearrange("p k (t q) -> p k t q", t=4),
                in_=w1s_raw[:, :, cols].rearrange("p k (q t) -> p k t q", t=4),
            )

        def squares(j):
            junk = work.tile([P, D], BF16, name="junk")
            nc.scalar.activation(
                out=junk[:], in_=x_sb[:, j, :], func=ACT.Square, scale=1.0 / 32, accum_out=ssq[:, j : j + 1]
            )

        def rho_rows(b):
            j0, n = BLOCKS[b][0] // P, BLOCKS[b][1] // P
            nc.gpsimd.tensor_tensor(
                out=rho[:, j0 : j0 + n], in0=ssq[:, j0 : j0 + n], in1=expo[:, 0:n], op=ALU.pow
            )
            ps = ypool.tile([P, 512], F32, name="y")
            for i in range(n):
                nc.tensor.matmul(
                    ps[:, P * i : P * i + P],
                    lhsT=rho[:, j0 + i : j0 + i + 1].to_broadcast([P, P]),
                    rhs=ident[:],
                    start=True,
                    stop=True,
                )
            nc.scalar.copy(out=rho_bc[:, P * j0 : P * (j0 + n)], in_=ps[:, 0 : P * n])

        def residual(j):
            for h in range(2):
                w = D // 2
                cols = slice(w * h, w * h + w)
                nc.gpsimd.tensor_tensor(out=xb[:, j, cols], in0=x_sb[:, j, cols], in1=b2h[:, cols], op=ALU.add)

        def spread_constants_c():
            nc.vector.tensor_copy(out=ident16[:], in_=ident[:])
            nc.tensor.matmul(
                c_ps[:].rearrange("p g t -> p (g t)"),
                lhsT=ident16[:], rhs=c_sb[:].rearrange("p g t -> p (g t)"), start=True, stop=True,
            )
            nc.scalar.copy(out=c32[:], in_=c_ps[:])

        def spread_constants():
            for h in range(2):
                cols = slice(512 * h, 512 * h + 512)
                ps = ypool.tile([P, 512], F32, name="y")
                nc.tensor.matmul(ps[:], lhsT=sel[:, 0, :], rhs=rows[:, 0, cols], start=True, stop=True)
                nc.scalar.copy(out=b2h[:, cols], in_=ps[:])
            for h in range(2):
                cols = slice(512 * h, 512 * h + 512)
                ps = ypool.tile([P, 512], F32, name="y")
                nc.tensor.matmul(ps[:], lhsT=sel[:, 2, :], rhs=rows[:, 2, cols], start=True, stop=True)
                nc.scalar.copy(out=beta_bc[:, cols], in_=ps[:])
            for h in range(2):
                cols = slice(512 * h, 512 * h + 512)
                nc.tensor.matmul(gain_ps[:, cols], lhsT=sel[:, 1, :], rhs=rows[:, 1, cols], start=True, stop=True)

        live = {}
        steps = [(b, g) for b in range(len(BLOCKS)) for g in range(G)]
        last = len(steps)

        def mm1(s):
            b, g = steps[s]
            m0, nb = BLOCKS[b]
            per = 512 // nb
            for h in range(4 // per):
                u = upool.tile([P, 512], F32, name="u")
                live["u", s, h] = u
                for i in range(per):
                    t = per * h + i
                    for k in range(K1):
                        nc.tensor.matmul_mx(
                            out=u[:, nb * i : nb * i + nb],
                            lhsT=w1_st[:, g, k, 256 * t : 256 * t + 256].bitcast(FP4),
                            lhsT_scale=w1s_st[:, g, k, 128 * t : 128 * t + 128],
                            rhs=x4_sb[:, m0 // 512, k, 2 * (m0 % 512) : 2 * (m0 % 512) + 2 * nb].bitcast(FP4),
                            rhs_scale=x4s[:, k, m0 : m0 + nb],
                            start=(k == 0),
                            stop=(k == K1 - 1),
                        )

        def scale_rows(s):
            b, g = steps[s]
            m0, nb = BLOCKS[b]
            per = 512 // nb
            v = work.tile([P, 4, nb], F32, name="v")
            live["v", s] = v
            r = rho_bc[:, m0 : m0 + nb].unsqueeze(1).to_broadcast([P, per, nb])
            for h in range(4 // per):
                nc.vector.tensor_tensor(
                    out=v[:, per * h : per * h + per, :],
                    in0=live.pop(("u", s, h))[:].rearrange("p (t n) -> p t n", t=per),
                    in1=r,
                    op=ALU.mult,
                )

        def swish(s):
            b, g = steps[s]
            nb = BLOCKS[b][1]
            v = live.pop(("v", s))
            w = work.tile([P, 4, nb], F32, name="w")
            live["w", s] = w
            for t in range(4):
                nc.scalar.activation(out=w[:, t, :], in_=v[:, t, :], func=ACT.Silu, bias=b1_sb[:, g, t : t + 1])

        def times_c(s):
            b, g = steps[s]
            nb = BLOCKS[b][1]
            w = live.pop(("w", s))
            h = work.tile([P, nb, 4], BF16, name="h", align_bytes=64)
            live["h", s] = h
            nc.vector.tensor_tensor(
                out=h[:].rearrange("p (a i) t -> p a t i", i=4),
                in0=w[:].rearrange("p t (a i) -> p a t i", i=4),
                in1=c_ps[:, g, :].unsqueeze(1).unsqueeze(3).to_broadcast([P, nb // 4, 4, 4]),
                op=ALU.mult,
            )

        def times_c_gp(s):
            b, g = steps[s]
            nb = BLOCKS[b][1]
            w = live.pop(("w", s))
            hc = work.tile([P, 4, nb], BF16, name="hc", align_bytes=64)
            live["hc", s] = hc
            for t in range(4):
                nc.gpsimd.tensor_scalar(
                    out=hc[:, t, :], in0=w[:, t, :], scalar1=c32[:, g, t : t + 1], scalar2=0.0, op0=ALU.mult, op1=ALU.add
                )

        def interleave(s):
            nb = BLOCKS[steps[s][0]][1]
            h = work.tile([P, nb, 4], BF16, name="h", align_bytes=64)
            live["h", s] = h
            nc.scalar.copy(
                out=h[:].rearrange("p (a i) t -> p a t i", i=4),
                in_=live.pop(("hc", s))[:].rearrange("p t (a i) -> p a t i", i=4),
            )

        def quantize(s):
            b, g = steps[s]
            nb = BLOCKS[b][1]
            if g == 0:
                live["codes", b] = work.tile([P, G, nb], U32, name="codes", align_bytes=64)
                live["scales", b] = work.tile([P, G, nb], U8, name="scales", align_bytes=64)
            nc.vector.quantize_mx(
                out=live["codes", b][:, g, :].bitcast(FP8),
                scales=live["scales", b][:, g, :],
                in_=live.pop(("h", s))[:].rearrange("p n t -> p (n t)"),
            )

        def mm2(j, gs):
            b, i = tile_of[j]
            for h in range(2):
                if gs[0] == 0:
                    live["y", j, h] = ypool.tile([P, 512], F32, name="y")
                for g in gs:
                    nc.tensor.matmul_mx(
                        out=live["y", j, h][:],
                        lhsT=live["codes", b][:, g, P * i : P * i + P].bitcast(FP8),
                        lhsT_scale=live["scales", b][:, g, P * i : P * i + P],
                        rhs=w2_sb[:, g, 1024 * h : 1024 * h + 1024].bitcast(FP4),
                        rhs_scale=w2s[:, g, 512 * h : 512 * h + 512],
                        start=(g == 0),
                        stop=(g == G - 1),
                    )

        def residual_sum(j):
            z = work.tile([P, D], F32, name="z")
            zs = work.tile([P, 8], F32, name="zs")
            nmu = work.tile([P, 8], F32, name="nmu")
            for h in range(2):
                cols = slice(512 * h, 512 * h + 512)
                nc.vector.scalar_tensor_tensor(
                    out=z[:, cols], in0=live.pop(("y", j, h))[:], scalar=0.5, in1=xb[:, j, cols],
                    op0=ALU.mult, op1=ALU.add, accum_out=zs[:, h : h + 1],
                )
            nc.vector.tensor_scalar(
                out=nmu[:, 0:1], in0=zs[:, 0:1], scalar1=zs[:, 1:2], scalar2=-1.0 / D, op0=ALU.add, op1=ALU.mult
            )
            live["z", j] = z
            live["nmu", j] = nmu

        def variance(j):
            junk = work.tile([P, D], F32, name="junkz")
            sq = work.tile([P, 8], F32, name="sq")
            rs = work.tile([P, 8], F32, name="rs")
            nmu = live.pop(("nmu", j))
            nc.scalar.activation(
                out=junk[:], in_=live["z", j][:], func=ACT.Square, bias=nmu[:, 0:1], accum_out=sq[:, 0:1]
            )
            nc.gpsimd.tensor_tensor(out=rs[:, 0:1], in0=sq[:, 0:1], in1=expo[:, 0:1], op=ALU.pow)
            if j in ON_VECTOR:
                live["rs", j] = rs
                live["nmu", j] = nmu
            else:
                nc.gpsimd.tensor_tensor(out=rs[:, 1:2], in0=rs[:, 0:1], in1=nmu[:, 0:1], op=ALU.mult)
                live["rs", j] = rs

        def normalize(j):
            xh = work.tile([P, D], F32, name="xh")
            rs = live.pop(("rs", j))
            nc.scalar.activation(
                out=xh[:], in_=live.pop(("z", j))[:], func=ACT.Identity, scale=rs[:, 0:1], bias=rs[:, 1:2]
            )
            live["xh", j] = xh

        def times_gain(j):
            xg = work.tile([P, D], F32, name="xg")
            nc.vector.tensor_tensor(out=xg[:], in0=live.pop(("xh", j))[:], in1=gain_ps[:], op=ALU.mult)
            live["xg", j] = xg

        def plus_beta(j):
            o = work.tile([P, D], F32, name="o")
            xg = live.pop(("xg", j))
            for h in range(2):
                cols = slice(512 * h, 512 * h + 512)
                nc.gpsimd.tensor_tensor(out=o[:, cols], in0=xg[:, cols], in1=beta_bc[:, cols], op=ALU.add)
                if j == TILES - 1:
                    nc.sync.dma_start(out=out_v[:, j, cols], in_=o[:, cols])
            if j < TILES - 1:
                nc.sync.dma_start(out=out_v[:, j, :], in_=o[:])

        def finish_on_vector(j):
            rs = live.pop(("rs", j))
            z = live.pop(("z", j))
            xg = work.tile([P, D], F32, name="xg")
            o = work.tile([P, D], F32, name="o")
            for h in range(2):
                cols = slice(512 * h, 512 * h + 512)
                nc.vector.scalar_tensor_tensor(
                    out=xg[:, cols], in0=z[:, cols], scalar=live.pop(("nmu", j))[:, 0:1] if h else live["nmu", j][:, 0:1], in1=gain_ps[:, cols], op0=ALU.add, op1=ALU.mult
                )
            for h in range(2):
                cols = slice(512 * h, 512 * h + 512)
                nc.vector.scalar_tensor_tensor(
                    out=o[:, cols], in0=xg[:, cols], scalar=rs[:, 0:1], in1=beta_bc[:, cols], op0=ALU.mult, op1=ALU.add
                )
                nc.sync.dma_start(out=out_v[:, j, cols], in_=o[:, cols])

        tile_of = {}
        for b, (m0, nb) in enumerate(BLOCKS):
            for i in range(nb // P):
                tile_of[m0 // P + i] = (b, i)

        plan = {}

        def at(step, fn, *args):
            plan.setdefault(max(step, 0), []).append((fn, args))

        slot = 0
        for j in range(TILES):
            b, i = tile_of[j]
            s0 = G * b
            e = s0 + G + 2
            zstep = max(e + 1 + i, slot)
            slot = zstep + 1
            if b > 0:
                at(s0 - 4 + i, squares, j)
            at(zstep - 4, residual, j)
            at(max(zstep - 1, e), mm2, j, range(G))
            at(zstep, residual_sum, j)
            at(zstep, variance, j)
            if j in ON_VECTOR:
                at(zstep + 1, finish_on_vector, j)
                continue
            at(zstep + 1, normalize, j)
            at(zstep + 2, times_gain, j)
            at(zstep + 2, plus_beta, j)
        for b in range(1, len(BLOCKS)):
            at(G * b - 2, rho_rows, b)

        for j in range(BLOCKS[0][1] // P):
            squares(j)
        permute_w1(0)
        rho_rows(0)
        spread_constants_c()
        spread_constants()
        mm1(0)
        permute_w1(1)

        for s in range(last + 14):
            early = [f for f in plan.get(s, []) if f[0] in (mm2,)]
            late = [f for f in plan.get(s, []) if f[0] not in (mm2,)]
            for fn, args in early:
                fn(*args)
            if s + 1 < last:
                mm1(s + 1)
            if s < last:
                scale_rows(s)
                swish(s)
            if 0 <= s - 1 < last and (s - 1) in GP_STEPS:
                times_c_gp(s - 1)
                interleave(s - 1)
            for fn, args in late:
                fn(*args)
            if s < 2:
                permute_w1(s + 2)
            if 0 <= s - 1 < last and (s - 1) not in GP_STEPS:
                times_c(s - 1)
            if 0 <= s - 2 < last:
                quantize(s - 2)
